import numpy as np
import ml_dtypes


def mxq(x, axis, fmt="e4m3"):
    dtype, down = {"e4m3": (ml_dtypes.float8_e4m3fn, 7), "e5m2": (ml_dtypes.float8_e5m2, 14)}[fmt]
    v = np.moveaxis(np.asarray(x, np.float32).astype(ml_dtypes.bfloat16).astype(np.float64), axis, -1)
    blocks = v.reshape(v.shape[:-1] + (-1, 32))
    amax = np.abs(blocks).max(-1, keepdims=True)
    byte = np.maximum(np.where(amax > 0, np.frexp(amax)[1] - 1 + 127, 0) - down, 1)
    scale = np.exp2(byte - 127.0)
    codes = (blocks / scale).astype(np.float32).astype(dtype).astype(np.float64)
    return np.moveaxis((codes * scale).reshape(v.shape), -1, axis)


WIDE = False


def mx_kscale(k):
    if not WIDE:
        return np.ones(k)
    levels = np.array([10, -10, 5, -5, 0])
    if k % 512:
        return np.exp2(np.random.permutation(np.resize(levels, k // 32))).repeat(32)
    a = np.empty((k // 512, 16))
    for p in range(k // 512):
        a[p, :8] = np.random.permutation(np.resize(levels, 8))
        for g in range(8):
            far = levels[np.abs(levels - a[p, g]) >= 10]
            a[p, g + 8] = far[np.random.randint(len(far))]
    return np.exp2(a.ravel()).repeat(32)


def f64(x):
    return np.asarray(x).astype(np.float64)


def striped(idx):
    return np.tile(np.asarray(idx).reshape(-1, 16).T, (8, 1)).astype(np.uint16)


def unstriped(offs):
    return offs[:16].T.reshape(-1).astype(np.int64)


B, N, T, D, DV, NQ = 1, 1024, 4096, 512, 128, 256


def setup_inputs():
    n = np.random.standard_normal
    idx = np.random.permutation(T)[:B * N]
    s = mx_kscale(D)[:, None]
    u = np.ones(T)
    u[idx] = mx_kscale(B * N)
    r = np.random.uniform(0.5, 2.0, T)
    k = n((D, T)) / s
    v = n((DV, T)) / (u * r)
    return {
        "qT": (n((B, D, NQ)) * s * (1.00 / np.sqrt(D))).astype(np.float32),
        "kT": k.astype(np.float32),
        "vT": v.astype(np.float32),
        "vs": np.tile(u * r, (128, 1)).astype(np.float32),
        "kb": np.tile(n(T), (128, 1)).astype(np.float32),
        "og": n((B, NQ, DV)).astype(np.float32),
        "offs": striped(idx),
    }


def reference(qT, kT, vT, vs, kb, og, offs):
    idx = unstriped(offs)
    k = f64(kT)
    v = f64(vT)
    pick = lambda x: x[:, idx].reshape(x.shape[0], B, N).transpose(1, 0, 2)
    q = f64(qT)
    score = mxq(q, 1, "e4m3").transpose(0, 2, 1) @ mxq(pick(k), 1, "e4m3")
    score = score + pick(f64(kb))[:, :1, :]
    p = score / (1.0 + np.exp(-score))
    w = p * pick(f64(vs))[:, :1, :]
    y = mxq(w, 2, "e4m3") @ mxq(pick(v).transpose(0, 2, 1), 1, "e4m3")
    y = y / 16.0
    y = y / (1.0 + np.exp(-f64(og)))
    return y

@@ -1,0 +1,198 @@
+from contextlib import ExitStack
+
+import concourse.mybir as mybir
+from concourse.masks import make_identity
+
+QUERIES = 256
+FEATURES = 512
+SLOTS = 1024
+TOKENS = 4096
+V_FEATURES = 128
+
+FLOPS = 2 * QUERIES * SLOTS * (FEATURES + V_FEATURES)
+
+F32 = mybir.dt.float32
+BF16 = mybir.dt.bfloat16
+U32 = mybir.dt.uint32
+U16 = mybir.dt.uint16
+U8 = mybir.dt.uint8
+FP8X4 = mybir.dt.float8_e4m3fn_x4
+
+COPY = mybir.ActivationFunctionType.Copy
+SIGMOID = mybir.ActivationFunctionType.Sigmoid
+SILU = mybir.ActivationFunctionType.Silu
+MULT = mybir.AluOpType.mult
+
+P = 128
+PACK = 4
+PASS = P * PACK
+PASSES = SLOTS // PASS
+Q_BLOCKS = QUERIES // P
+
+
+def tile_attend_silu_gate_kernel(tc, qT, kT, vT, vs, kb, og, offs, out):
+    nc = tc.nc
+    with ExitStack() as ctx:
+        keep = ctx.enter_context(tc.tile_pool(name="keep", bufs=1))
+        half = ctx.enter_context(tc.tile_pool(name="half", bufs=2))
+        turn_psum = ctx.enter_context(tc.psum_pool(name="turn_psum", bufs=2))
+        score_psum = ctx.enter_context(tc.psum_pool(name="score_psum", bufs=4))
+        y_psum = ctx.enter_context(tc.psum_pool(name="y_psum", bufs=2))
+
+        offsets = keep.tile([P, SLOTS // 16], U16, name="offsets")
+        ident = keep.tile([P, P], F32, name="ident")
+        kb_row = keep.tile([P, TOKENS], F32, name="kb_row")
+        vs_row = keep.tile([P, TOKENS], F32, name="vs_row")
+        k_planes = [keep.tile([P, TOKENS], F32, name="k_plane%d" % j) for j in range(PACK)]
+        v_pool = keep.tile([P, TOKENS], F32, name="v_pool")
+        q_raw = keep.tile([P, PACK, QUERIES], F32, name="q_raw")
+        gate_in = keep.tile([P, Q_BLOCKS, V_FEATURES], F32, name="gate_in")
+
+        k_rows = kT.rearrange("(p j) n -> j p n", j=PACK)
+
+        middle = TOKENS // 2
+        nc.vector.memset(kb_row[:, 0:middle], 0.0)
+        nc.gpsimd.memset(kb_row[:, middle:TOKENS], 0.0)
+        nc.vector.memset(vs_row[:, 0:middle], 0.0)
+        nc.gpsimd.memset(vs_row[:, middle:TOKENS], 0.0)
+        make_identity(nc, ident[:])
+        nc.scalar.dma_start(gate_in[:], og[0].rearrange("(b p) e -> p b e", p=P))
+        nc.sync.dma_start(offsets[:], offs)
+        nc.sync.dma_start(q_raw[:], qT[0].rearrange("(p j) q -> p j q", j=PACK))
+        nc.sync.dma_start(kb_row[0:1, :], kb[0:1, :])
+        nc.sync.dma_start(k_planes[0][:], k_rows[0])
+        nc.sync.dma_start(vs_row[0:1, :], vs[0:1, :])
+        for j in range(1, PACK):
+            nc.sync.dma_start(k_planes[j][:], k_rows[j])
+        nc.sync.dma_start(v_pool[:], vT)
+
+        gate = keep.tile([P, Q_BLOCKS, V_FEATURES], F32, name="gate")
+        nc.scalar.activation(gate[:], gate_in[:], SIGMOID)
+        warm = keep.tile([P, 1], F32, name="warm")
+        nc.scalar.activation(warm[:], gate[:, 0, 0:1], SILU)
+
+        k_packed = keep.tile([P, PASSES, PACK, P, PACK], BF16, name="k_packed", align_bytes=64)
+        k_codes = keep.tile([P, SLOTS], U32, name="k_codes", align_bytes=64)
+        k_scales = keep.tile([P, SLOTS], U8, name="k_scales", align_bytes=64)
+
+        def gather_keys(j):
+            nc.vector.tensor_copy(
+                k_packed[:, :, :, :, j].rearrange("p g t m -> p g m t"),
+                k_planes[j][:].indirect(offsets[:]),
+            )
+
+        def gather_keys_half(j, g):
+            nc.vector.tensor_copy(
+                k_packed[:, g, :, :, j].rearrange("p t m -> p m t"),
+                k_planes[j][:].indirect(offsets[:, 32 * g : 32 * g + 32]),
+            )
+
+        def columns(row, name):
+            picked = keep.tile([P, SLOTS], F32, name=name + "_picked")
+            nc.vector.tensor_copy(picked[:], row[:].indirect(offsets[:]))
+            cols = keep.tile([P, PASSES, PACK], F32, name=name + "_cols")
+            for g in range(PASSES):
+                turned = turn_psum.tile([P, PACK, P], F32, name="turned")
+                for t in range(PACK):
+                    nc.tensor.transpose(turned[:, t, :], picked[:, PASS * g + t : PASS * (g + 1) : PACK], ident[:])
+                nc.scalar.copy(cols[:, g, :], turned[:, :, 0])
+            return cols
+
+        kb_cols = columns(kb_row, "kb")
+        gather_keys(0)
+        vs_cols = columns(vs_row, "vs")
+
+        q_packed = keep.tile([P, QUERIES, PACK], BF16, name="q_packed", align_bytes=64)
+        q_codes = keep.tile([P, QUERIES], U32, name="q_codes", align_bytes=64)
+        q_scales = keep.tile([P, QUERIES], U8, name="q_scales", align_bytes=64)
+        nc.scalar.copy(q_packed[:], q_raw[:].rearrange("p j q -> p q j"))
+
+        gather_keys(1)
+        nc.vector.quantize_mx(
+            out=q_codes[:].bitcast(FP8X4), scales=q_scales[:], in_=q_packed[:].rearrange("p q j -> p (q j)")
+        )
+        gather_keys(2)
+        for g in range(PASSES):
+            gather_keys_half(3, g)
+        for g in range(PASSES):
+            cols = slice(PASS * g, PASS * (g + 1))
+            nc.vector.quantize_mx(
+                out=k_codes[:, cols].bitcast(FP8X4),
+                scales=k_scales[:, cols],
+                in_=k_packed[:, g, :, :, :].rearrange("p t m j -> p (t m j)"),
+            )
+
+        p_tiles = []
+        for g in range(PASSES):
+            p_tile = half.tile([P, PACK, QUERIES], F32, name="p_tile")
+            p_tiles.append(p_tile)
+            for pair in range(2):
+                bank = score_psum.tile([P, 2, QUERIES], F32, name="bank")
+                for i in range(2):
+                    c0 = PASS * g + P * (2 * pair + i)
+                    nc.tensor.matmul_mx(
+                        out=bank[:, i, :],
+                        lhsT=k_codes[:, c0 : c0 + P].bitcast(FP8X4),
+                        lhsT_scale=k_scales[:, c0 : c0 + P],
+                        rhs=q_codes[:].bitcast(FP8X4),
+                        rhs_scale=q_scales[:],
+                        start=True,
+                        stop=True,
+                    )
+                for i in range(2):
+                    t = 2 * pair + i
+                    nc.scalar.activation(p_tile[:, t, :], bank[:, i, :], SILU, bias=kb_cols[:, g, t : t + 1])
+
+        w_codes = keep.tile([P, PASSES, QUERIES], U32, name="w_codes", align_bytes=64)
+        w_scales = keep.tile([P, PASSES, QUERIES], U8, name="w_scales", align_bytes=64)
+        v_codes = keep.tile([P, PASSES, V_FEATURES], U32, name="v_codes", align_bytes=64)
+        v_scales = keep.tile([P, PASSES, V_FEATURES], U8, name="v_scales", align_bytes=64)
+
+        w_tiles = []
+        v_tiles = []
+        for g in range(PASSES):
+            v_picked = half.tile([P, PASS], F32, name="v_picked")
+            nc.vector.tensor_copy(v_picked[:], v_pool[:].indirect(offsets[:, 32 * g : 32 * g + 32]))
+            turned = turn_psum.tile([P, PACK, P], F32, name="turned")
+            for t in range(PACK):
+                nc.tensor.transpose(turned[:, t, :], v_picked[:, t:PASS:PACK], ident[:])
+            v_packed = half.tile([P, V_FEATURES, PACK], BF16, name="v_packed", align_bytes=64)
+            nc.scalar.copy(v_packed[:], turned[:].rearrange("p t e -> p e t"))
+            v_tiles.append(v_packed)
+            w_packed = half.tile([P, QUERIES, PACK], BF16, name="w_packed", align_bytes=64)
+            nc.vector.tensor_tensor(
+                w_packed[:],
+                p_tiles[g][:].rearrange("p t q -> p q t"),
+                vs_cols[:, g, :].unsqueeze(1).to_broadcast([P, QUERIES, PACK]),
+                MULT,
+            )
+            w_tiles.append(w_packed)
+        for g in range(PASSES):
+            nc.vector.quantize_mx(
+                out=w_codes[:, g, :].bitcast(FP8X4),
+                scales=w_scales[:, g, :],
+                in_=w_tiles[g][:].rearrange("p q t -> p (q t)"),
+            )
+            nc.vector.quantize_mx(
+                out=v_codes[:, g, :].bitcast(FP8X4),
+                scales=v_scales[:, g, :],
+                in_=v_tiles[g][:].rearrange("p e t -> p (e t)"),
+            )
+
+        for b in range(Q_BLOCKS):
+            q_cols = slice(P * b, P * (b + 1))
+            y = y_psum.tile([P, V_FEATURES], F32, name="y")
+            for g in range(PASSES):
+                nc.tensor.matmul_mx(
+                    out=y[:],
+                    lhsT=w_codes[:, g, q_cols].bitcast(FP8X4),
+                    lhsT_scale=w_scales[:, g, q_cols],
+                    rhs=v_codes[:, g, :].bitcast(FP8X4),
+                    rhs_scale=v_scales[:, g, :],
+                    start=(g == 0),
+                    stop=(g == PASSES - 1),
+                )
+            result = half.tile([P, V_FEATURES], F32, name="result")
+            nc.vector.scalar_tensor_tensor(result[:], y[:], 1.0 / 16.0, gate[:, b, :], MULT, MULT)
+            queue = nc.sync if b == 0 else nc.scalar
+            queue.dma_start(out[0, q_cols, :], result[:])

@@ -26,6 +26,7 @@ MULT = mybir.AluOpType.mult
 P = 128
 PACK = 4
 PASS = P * PACK
+RUN = 8
 PASSES = SLOTS // PASS
 Q_BLOCKS = QUERIES // P
 
@@ -41,6 +42,7 @@ def tile_attend_silu_gate_kernel(tc, qT, kT, vT, vs, kb, og, offs, out):
 
         offsets = keep.tile([P, SLOTS // 16], U16, name="offsets")
         ident = keep.tile([P, P], F32, name="ident")
+        ident_bf = keep.tile([P, P], BF16, name="ident_bf")
         kb_row = keep.tile([P, TOKENS], F32, name="kb_row")
         vs_row = keep.tile([P, TOKENS], F32, name="vs_row")
         k_planes = [keep.tile([P, TOKENS], F32, name="k_plane%d" % j) for j in range(PACK)]
@@ -56,14 +58,16 @@ def tile_attend_silu_gate_kernel(tc, qT, kT, vT, vs, kb, og, offs, out):
         nc.vector.memset(vs_row[:, 0:middle], 0.0)
         nc.gpsimd.memset(vs_row[:, middle:TOKENS], 0.0)
         make_identity(nc, ident[:])
+        nc.gpsimd.tensor_copy(ident_bf[:], ident[:])
         nc.scalar.dma_start(gate_in[:], og[0].rearrange("(b p) e -> p b e", p=P))
         nc.sync.dma_start(offsets[:], offs)
-        nc.sync.dma_start(q_raw[:], qT[0].rearrange("(p j) q -> p j q", j=PACK))
+        nc.sync.dma_start(k_planes[0][:, 0:middle], k_rows[0, :, 0:middle])
         nc.sync.dma_start(kb_row[0:1, :], kb[0:1, :])
-        nc.sync.dma_start(k_planes[0][:], k_rows[0])
+        nc.sync.dma_start(k_planes[0][:, middle:TOKENS], k_rows[0, :, middle:TOKENS])
         nc.sync.dma_start(vs_row[0:1, :], vs[0:1, :])
         for j in range(1, PACK):
             nc.sync.dma_start(k_planes[j][:], k_rows[j])
+        nc.sync.dma_start(q_raw[:], qT[0].rearrange("(p j) q -> p j q", j=PACK))
         nc.sync.dma_start(v_pool[:], vT)
 
         gate = keep.tile([P, Q_BLOCKS, V_FEATURES], F32, name="gate")
@@ -75,46 +79,44 @@ def tile_attend_silu_gate_kernel(tc, qT, kT, vT, vs, kb, og, offs, out):
         k_codes = keep.tile([P, SLOTS], U32, name="k_codes", align_bytes=64)
         k_scales = keep.tile([P, SLOTS], U8, name="k_scales", align_bytes=64)
 
-        def gather_keys(j):
+        def gather_keys(j, g):
             nc.vector.tensor_copy(
-                k_packed[:, :, :, :, j].rearrange("p g t m -> p g m t"),
-                k_planes[j][:].indirect(offsets[:]),
-            )
-
-        def gather_keys_half(j, g):
-            nc.vector.tensor_copy(
-                k_packed[:, g, :, :, j].rearrange("p t m -> p m t"),
+                k_packed[:, g, :, :, j].rearrange("p t (b i) -> p b t i", i=RUN),
                 k_planes[j][:].indirect(offsets[:, 32 * g : 32 * g + 32]),
             )
 
         def columns(row, name):
             picked = keep.tile([P, SLOTS], F32, name=name + "_picked")
             nc.vector.tensor_copy(picked[:], row[:].indirect(offsets[:]))
+            ordered = keep.tile([P, PASSES, PACK, P], F32, name=name + "_ordered")
+            for g in range(PASSES):
+                nc.scalar.copy(
+                    ordered[:, g].rearrange("p t (b i) -> p t b i", i=RUN),
+                    picked[:, PASS * g : PASS * (g + 1)].rearrange("p (b t i) -> p t b i", t=PACK, i=RUN),
+                )
             cols = keep.tile([P, PASSES, PACK], F32, name=name + "_cols")
             for g in range(PASSES):
-                turned = turn_psum.tile([P, PACK, P], F32, name="turned")
+                turned = turn_psum.tile([P, PACK, P], F32, name="turned", tag="turned")
                 for t in range(PACK):
-                    nc.tensor.transpose(turned[:, t, :], picked[:, PASS * g + t : PASS * (g + 1) : PACK], ident[:])
+                    nc.tensor.transpose(turned[:, t, :], ordered[:, g, t, :], ident[:])
                 nc.scalar.copy(cols[:, g, :], turned[:, :, 0])
             return cols
 
         kb_cols = columns(kb_row, "kb")
-        gather_keys(0)
+        for g in range(PASSES):
+            gather_keys(0, g)
         vs_cols = columns(vs_row, "vs")
+
+        for j in range(1, PACK - 1):
+            for g in range(PASSES):
+                gather_keys(j, g)
 
         q_packed = keep.tile([P, QUERIES, PACK], BF16, name="q_packed", align_bytes=64)
         q_codes = keep.tile([P, QUERIES], U32, name="q_codes", align_bytes=64)
         q_scales = keep.tile([P, QUERIES], U8, name="q_scales", align_bytes=64)
         nc.scalar.copy(q_packed[:], q_raw[:].rearrange("p j q -> p q j"))
 
-        gather_keys(1)
-        nc.vector.quantize_mx(
-            out=q_codes[:].bitcast(FP8X4), scales=q_scales[:], in_=q_packed[:].rearrange("p q j -> p (q j)")
-        )
-        gather_keys(2)
-        for g in range(PASSES):
-            gather_keys_half(3, g)
-        for g in range(PASSES):
+        def quantize_keys(g):
             cols = slice(PASS * g, PASS * (g + 1))
             nc.vector.quantize_mx(
                 out=k_codes[:, cols].bitcast(FP8X4),
@@ -122,10 +124,15 @@ def tile_attend_silu_gate_kernel(tc, qT, kT, vT, vs, kb, og, offs, out):
                 in_=k_packed[:, g, :, :, :].rearrange("p t m j -> p (t m j)"),
             )
 
-        p_tiles = []
-        for g in range(PASSES):
-            p_tile = half.tile([P, PACK, QUERIES], F32, name="p_tile")
-            p_tiles.append(p_tile)
+        p_tiles = [half.tile([P, PACK, QUERIES], F32, name="p_tile%d" % g) for g in range(PASSES)]
+        w_tiles = [half.tile([P, QUERIES, PACK], BF16, name="w_packed%d" % g, align_bytes=64) for g in range(PASSES)]
+        v_tiles = [half.tile([P, V_FEATURES, PACK], BF16, name="v_packed%d" % g, align_bytes=64) for g in range(PASSES)]
+        w_codes = keep.tile([P, PASSES, QUERIES], U32, name="w_codes", align_bytes=64)
+        w_scales = keep.tile([P, PASSES, QUERIES], U8, name="w_scales", align_bytes=64)
+        v_codes = keep.tile([P, PASSES, V_FEATURES], U32, name="v_codes", align_bytes=64)
+        v_scales = keep.tile([P, PASSES, V_FEATURES], U8, name="v_scales", align_bytes=64)
+
+        def score(g):
             for pair in range(2):
                 bank = score_psum.tile([P, 2, QUERIES], F32, name="bank")
                 for i in range(2):
@@ -141,43 +148,58 @@ def tile_attend_silu_gate_kernel(tc, qT, kT, vT, vs, kb, og, offs, out):
                     )
                 for i in range(2):
                     t = 2 * pair + i
-                    nc.scalar.activation(p_tile[:, t, :], bank[:, i, :], SILU, bias=kb_cols[:, g, t : t + 1])
+                    nc.scalar.activation(p_tiles[g][:, t, :], bank[:, i, :], SILU, bias=kb_cols[:, g, t : t + 1])
 
-        w_codes = keep.tile([P, PASSES, QUERIES], U32, name="w_codes", align_bytes=64)
-        w_scales = keep.tile([P, PASSES, QUERIES], U8, name="w_scales", align_bytes=64)
-        v_codes = keep.tile([P, PASSES, V_FEATURES], U32, name="v_codes", align_bytes=64)
-        v_scales = keep.tile([P, PASSES, V_FEATURES], U8, name="v_scales", align_bytes=64)
-
-        w_tiles = []
-        v_tiles = []
-        for g in range(PASSES):
-            v_picked = half.tile([P, PASS], F32, name="v_picked")
-            nc.vector.tensor_copy(v_picked[:], v_pool[:].indirect(offsets[:, 32 * g : 32 * g + 32]))
-            turned = turn_psum.tile([P, PACK, P], F32, name="turned")
-            for t in range(PACK):
-                nc.tensor.transpose(turned[:, t, :], v_picked[:, t:PASS:PACK], ident[:])
-            v_packed = half.tile([P, V_FEATURES, PACK], BF16, name="v_packed", align_bytes=64)
-            nc.scalar.copy(v_packed[:], turned[:].rearrange("p t e -> p e t"))
-            v_tiles.append(v_packed)
-            w_packed = half.tile([P, QUERIES, PACK], BF16, name="w_packed", align_bytes=64)
+        def weigh(g):
             nc.vector.tensor_tensor(
-                w_packed[:],
+                w_tiles[g][:],
                 p_tiles[g][:].rearrange("p t q -> p q t"),
                 vs_cols[:, g, :].unsqueeze(1).to_broadcast([P, QUERIES, PACK]),
                 MULT,
             )
-            w_tiles.append(w_packed)
-        for g in range(PASSES):
+
+        def quantize_weights(g):
             nc.vector.quantize_mx(
                 out=w_codes[:, g, :].bitcast(FP8X4),
                 scales=w_scales[:, g, :],
                 in_=w_tiles[g][:].rearrange("p q t -> p (q t)"),
             )
+
+        def gather_values(g):
+            v_picked = half.tile([P, PACK, P], BF16, name="v_picked")
+            nc.vector.tensor_copy(
+                v_picked[:].rearrange("p t (b i) -> p b t i", i=RUN),
+                v_pool[:].indirect(offsets[:, 32 * g : 32 * g + 32]),
+            )
+            turned = turn_psum.tile([P, PACK, P], BF16, name="turned_v", tag="turned")
+            for t in range(PACK):
+                nc.tensor.transpose(turned[:, t, :], v_picked[:, t, :], ident_bf[:])
+            nc.scalar.copy(v_tiles[g][:], turned[:].rearrange("p t e -> p e t"))
+
+        def quantize_values(g):
             nc.vector.quantize_mx(
                 out=v_codes[:, g, :].bitcast(FP8X4),
                 scales=v_scales[:, g, :],
                 in_=v_tiles[g][:].rearrange("p e t -> p (e t)"),
             )
+
+        gather_keys(3, 0)
+        quantize_keys(0)
+        nc.vector.quantize_mx(
+            out=q_codes[:].bitcast(FP8X4), scales=q_scales[:], in_=q_packed[:].rearrange("p q j -> p (q j)")
+        )
+        score(0)
+        gather_keys(3, 1)
+        weigh(0)
+        quantize_keys(1)
+        score(1)
+        gather_values(0)
+        quantize_weights(0)
+        gather_values(1)
+        quantize_values(0)
+        weigh(1)
+        quantize_values(1)
+        quantize_weights(1)
 
         for b in range(Q_BLOCKS):
             q_cols = slice(P * b, P * (b + 1))

@@ -55,18 +55,19 @@ def tile_attend_silu_gate_kernel(tc, qT, kT, vT, vs, kb, og, offs, out):
         middle = TOKENS // 2
         nc.vector.memset(kb_row[:, 0:middle], 0.0)
         nc.gpsimd.memset(kb_row[:, middle:TOKENS], 0.0)
-        nc.vector.memset(vs_row[:, 0:middle], 0.0)
-        nc.gpsimd.memset(vs_row[:, middle:TOKENS], 0.0)
+        nc.gpsimd.memset(vs_row[:], 0.0)
         make_identity(nc, ident[:])
         nc.gpsimd.tensor_copy(ident_bf[:], ident[:])
         nc.scalar.dma_start(gate_in[:], og[0].rearrange("(b p) e -> p b e", p=P))
         nc.sync.dma_start(offsets[:], offs)
-        nc.sync.dma_start(k_planes[0][:, 0:middle], k_rows[0, :, 0:middle])
+        cut = 3 * TOKENS // 4
+        nc.sync.dma_start(k_planes[0][:, 0:cut], k_rows[0, :, 0:cut])
         nc.sync.dma_start(kb_row[0:1, :], kb[0:1, :])
-        nc.sync.dma_start(k_planes[0][:, middle:TOKENS], k_rows[0, :, middle:TOKENS])
+        nc.sync.dma_start(k_planes[0][:, cut:TOKENS], k_rows[0, :, cut:TOKENS])
+        nc.sync.dma_start(k_planes[1][:], k_rows[1])
         nc.sync.dma_start(vs_row[0:1, :], vs[0:1, :])
-        for j in range(1, PACK):
-            nc.sync.dma_start(k_planes[j][:], k_rows[j])
+        nc.sync.dma_start(k_planes[2][:], k_rows[2])
+        nc.sync.dma_start(k_planes[3][:], k_rows[3])
         nc.sync.dma_start(q_raw[:], qT[0].rearrange("(p j) q -> p j q", j=PACK))
         nc.sync.dma_start(v_pool[:], vT)
 
@@ -78,6 +79,12 @@ def tile_attend_silu_gate_kernel(tc, qT, kT, vT, vs, kb, og, offs, out):
         k_packed = keep.tile([P, PASSES, PACK, P, PACK], BF16, name="k_packed", align_bytes=64)
         k_codes = keep.tile([P, SLOTS], U32, name="k_codes", align_bytes=64)
         k_scales = keep.tile([P, SLOTS], U8, name="k_scales", align_bytes=64)
+
+        def gather_keys_whole(j):
+            nc.vector.tensor_copy(
+                k_packed[:, :, :, :, j].rearrange("p g t (b i) -> p g b t i", i=RUN),
+                k_planes[j][:].indirect(offsets[:]),
+            )
 
         def gather_keys(j, g):
             nc.vector.tensor_copy(
@@ -103,13 +110,11 @@ def tile_attend_silu_gate_kernel(tc, qT, kT, vT, vs, kb, og, offs, out):
             return cols
 
         kb_cols = columns(kb_row, "kb")
-        for g in range(PASSES):
-            gather_keys(0, g)
-        vs_cols = columns(vs_row, "vs")
+        gather_keys_whole(0)
 
-        for j in range(1, PACK - 1):
-            for g in range(PASSES):
-                gather_keys(j, g)
+        gather_keys_whole(1)
+        vs_cols = columns(vs_row, "vs")
+        gather_keys_whole(2)
 
         q_packed = keep.tile([P, QUERIES, PACK], BF16, name="q_packed", align_bytes=64)
         q_codes = keep.tile([P, QUERIES], U32, name="q_codes", align_bytes=64)

@@ -26,7 +26,6 @@ MULT = mybir.AluOpType.mult
 P = 128
 PACK = 4
 PASS = P * PACK
-RUN = 8
 PASSES = SLOTS // PASS
 Q_BLOCKS = QUERIES // P
 
@@ -42,7 +41,6 @@ def tile_attend_silu_gate_kernel(tc, qT, kT, vT, vs, kb, og, offs, out):
 
         offsets = keep.tile([P, SLOTS // 16], U16, name="offsets")
         ident = keep.tile([P, P], F32, name="ident")
-        ident_bf = keep.tile([P, P], BF16, name="ident_bf")
         kb_row = keep.tile([P, TOKENS], F32, name="kb_row")
         vs_row = keep.tile([P, TOKENS], F32, name="vs_row")
         k_planes = [keep.tile([P, TOKENS], F32, name="k_plane%d" % j) for j in range(PACK)]
@@ -52,23 +50,20 @@ def tile_attend_silu_gate_kernel(tc, qT, kT, vT, vs, kb, og, offs, out):
 
         k_rows = kT.rearrange("(p j) n -> j p n", j=PACK)
 
-        middle = TOKENS // 2
-        nc.vector.memset(kb_row[:, 0:middle], 0.0)
-        nc.gpsimd.memset(kb_row[:, middle:TOKENS], 0.0)
-        nc.gpsimd.memset(vs_row[:], 0.0)
+        share = 3 * TOKENS // 4
+        for row in (kb_row, vs_row):
+            nc.vector.memset(row[:, 0:share], 0.0)
+            nc.gpsimd.memset(row[:, share:TOKENS], 0.0)
         make_identity(nc, ident[:])
-        nc.gpsimd.tensor_copy(ident_bf[:], ident[:])
         nc.scalar.dma_start(gate_in[:], og[0].rearrange("(b p) e -> p b e", p=P))
         nc.sync.dma_start(offsets[:], offs)
-        cut = 3 * TOKENS // 4
-        nc.sync.dma_start(k_planes[0][:, 0:cut], k_rows[0, :, 0:cut])
+        nc.sync.dma_start(k_planes[0][:], k_rows[0])
         nc.sync.dma_start(kb_row[0:1, :], kb[0:1, :])
-        nc.sync.dma_start(k_planes[0][:, cut:TOKENS], k_rows[0, :, cut:TOKENS])
         nc.sync.dma_start(k_planes[1][:], k_rows[1])
         nc.sync.dma_start(vs_row[0:1, :], vs[0:1, :])
         nc.sync.dma_start(k_planes[2][:], k_rows[2])
-        nc.sync.dma_start(k_planes[3][:], k_rows[3])
         nc.sync.dma_start(q_raw[:], qT[0].rearrange("(p j) q -> p j q", j=PACK))
+        nc.sync.dma_start(k_planes[3][:], k_rows[3])
         nc.sync.dma_start(v_pool[:], vT)
 
         gate = keep.tile([P, Q_BLOCKS, V_FEATURES], F32, name="gate")
@@ -80,42 +75,47 @@ def tile_attend_silu_gate_kernel(tc, qT, kT, vT, vs, kb, og, offs, out):
         k_codes = keep.tile([P, SLOTS], U32, name="k_codes", align_bytes=64)
         k_scales = keep.tile([P, SLOTS], U8, name="k_scales", align_bytes=64)
 
-        def gather_keys_whole(j):
+        k_picked = keep.tile([P, 2, SLOTS], F32, name="k_picked")
+
+        def gather_keys_plain(j):
+            nc.vector.tensor_copy(k_picked[:, j, :], k_planes[j][:].indirect(offsets[:]))
+
+        def interleave_keys(g):
+            nc.scalar.copy(
+                k_packed[:, g, :, :, 0:2],
+                k_picked[:, :, PASS * g : PASS * (g + 1)].rearrange("p j (m t) -> p t m j", t=PACK),
+            )
+
+        def gather_keys(j):
             nc.vector.tensor_copy(
-                k_packed[:, :, :, :, j].rearrange("p g t (b i) -> p g b t i", i=RUN),
+                k_packed[:, :, :, :, j].rearrange("p g t m -> p g m t"),
                 k_planes[j][:].indirect(offsets[:]),
             )
 
-        def gather_keys(j, g):
+        def gather_keys_half(j, g):
             nc.vector.tensor_copy(
-                k_packed[:, g, :, :, j].rearrange("p t (b i) -> p b t i", i=RUN),
+                k_packed[:, g, :, :, j].rearrange("p t m -> p m t"),
                 k_planes[j][:].indirect(offsets[:, 32 * g : 32 * g + 32]),
             )
 
         def columns(row, name):
             picked = keep.tile([P, SLOTS], F32, name=name + "_picked")
             nc.vector.tensor_copy(picked[:], row[:].indirect(offsets[:]))
-            ordered = keep.tile([P, PASSES, PACK, P], F32, name=name + "_ordered")
-            for g in range(PASSES):
-                nc.scalar.copy(
-                    ordered[:, g].rearrange("p t (b i) -> p t b i", i=RUN),
-                    picked[:, PASS * g : PASS * (g + 1)].rearrange("p (b t i) -> p t b i", t=PACK, i=RUN),
-                )
             cols = keep.tile([P, PASSES, PACK], F32, name=name + "_cols")
             for g in range(PASSES):
                 turned = turn_psum.tile([P, PACK, P], F32, name="turned", tag="turned")
                 for t in range(PACK):
-                    nc.tensor.transpose(turned[:, t, :], ordered[:, g, t, :], ident[:])
+                    nc.tensor.transpose(turned[:, t, :], picked[:, PASS * g + t : PASS * (g + 1) : PACK], ident[:])
                 nc.scalar.copy(cols[:, g, :], turned[:, :, 0])
             return cols
 
+        gather_keys_plain(0)
         kb_cols = columns(kb_row, "kb")
-        gather_keys_whole(0)
-
-        gather_keys_whole(1)
+        gather_keys_plain(1)
+        for g in range(PASSES):
+            interleave_keys(g)
         vs_cols = columns(vs_row, "vs")
-        gather_keys_whole(2)
-
+        gather_keys(2)
         q_packed = keep.tile([P, QUERIES, PACK], BF16, name="q_packed", align_bytes=64)
         q_codes = keep.tile([P, QUERIES], U32, name="q_codes", align_bytes=64)
         q_scales = keep.tile([P, QUERIES], U8, name="q_scales", align_bytes=64)
@@ -130,7 +130,6 @@ def tile_attend_silu_gate_kernel(tc, qT, kT, vT, vs, kb, og, offs, out):
             )
 
         p_tiles = [half.tile([P, PACK, QUERIES], F32, name="p_tile%d" % g) for g in range(PASSES)]
-        w_tiles = [half.tile([P, QUERIES, PACK], BF16, name="w_packed%d" % g, align_bytes=64) for g in range(PASSES)]
         v_tiles = [half.tile([P, V_FEATURES, PACK], BF16, name="v_packed%d" % g, align_bytes=64) for g in range(PASSES)]
         w_codes = keep.tile([P, PASSES, QUERIES], U32, name="w_codes", align_bytes=64)
         w_scales = keep.tile([P, PASSES, QUERIES], U8, name="w_scales", align_bytes=64)
@@ -155,9 +154,13 @@ def tile_attend_silu_gate_kernel(tc, qT, kT, vT, vs, kb, og, offs, out):
                     t = 2 * pair + i
                     nc.scalar.activation(p_tiles[g][:, t, :], bank[:, i, :], SILU, bias=kb_cols[:, g, t : t + 1])
 
+        w_tiles = []
+
         def weigh(g):
+            w_packed = half.tile([P, QUERIES, PACK], BF16, name="w_packed", tag="stage", align_bytes=64)
+            w_tiles.append(w_packed)
             nc.vector.tensor_tensor(
-                w_tiles[g][:],
+                w_packed[:],
                 p_tiles[g][:].rearrange("p t q -> p q t"),
                 vs_cols[:, g, :].unsqueeze(1).to_broadcast([P, QUERIES, PACK]),
                 MULT,
@@ -171,14 +174,11 @@ def tile_attend_silu_gate_kernel(tc, qT, kT, vT, vs, kb, og, offs, out):
             )
 
         def gather_values(g):
-            v_picked = half.tile([P, PACK, P], BF16, name="v_picked")
-            nc.vector.tensor_copy(
-                v_picked[:].rearrange("p t (b i) -> p b t i", i=RUN),
-                v_pool[:].indirect(offsets[:, 32 * g : 32 * g + 32]),
-            )
-            turned = turn_psum.tile([P, PACK, P], BF16, name="turned_v", tag="turned")
+            v_picked = half.tile([P, PASS], F32, name="v_picked", tag="stage", align_bytes=64)
+            nc.vector.tensor_copy(v_picked[:], v_pool[:].indirect(offsets[:, 32 * g : 32 * g + 32]))
+            turned = turn_psum.tile([P, PACK, P], F32, name="turned_v", tag="turned")
             for t in range(PACK):
-                nc.tensor.transpose(turned[:, t, :], v_picked[:, t, :], ident_bf[:])
+                nc.tensor.transpose(turned[:, t, :], v_picked[:, t:PASS:PACK], ident[:])
             nc.scalar.copy(v_tiles[g][:], turned[:].rearrange("p t e -> p e t"))
 
         def quantize_values(g):
@@ -188,21 +188,21 @@ def tile_attend_silu_gate_kernel(tc, qT, kT, vT, vs, kb, og, offs, out):
                 in_=v_tiles[g][:].rearrange("p e t -> p (e t)"),
             )
 
-        gather_keys(3, 0)
-        quantize_keys(0)
         nc.vector.quantize_mx(
             out=q_codes[:].bitcast(FP8X4), scales=q_scales[:], in_=q_packed[:].rearrange("p q j -> p (q j)")
         )
+        gather_keys_half(3, 0)
+        gather_keys_half(3, 1)
+        quantize_keys(0)
         score(0)
-        gather_keys(3, 1)
-        weigh(0)
         quantize_keys(1)
         score(1)
         gather_values(0)
-        quantize_weights(0)
         gather_values(1)
-        quantize_values(0)
+        weigh(0)
         weigh(1)
+        quantize_weights(0)
+        quantize_values(0)
         quantize_values(1)
         quantize_weights(1)
 

from contextlib import ExitStack

import concourse.mybir as mybir
from concourse.masks import make_identity

QUERIES = 256
FEATURES = 512
SLOTS = 1024
TOKENS = 4096
V_FEATURES = 128

FLOPS = 2 * QUERIES * SLOTS * (FEATURES + V_FEATURES)

F32 = mybir.dt.float32
BF16 = mybir.dt.bfloat16
U32 = mybir.dt.uint32
U16 = mybir.dt.uint16
U8 = mybir.dt.uint8
FP8X4 = mybir.dt.float8_e4m3fn_x4

COPY = mybir.ActivationFunctionType.Copy
SIGMOID = mybir.ActivationFunctionType.Sigmoid
SILU = mybir.ActivationFunctionType.Silu
MULT = mybir.AluOpType.mult

P = 128
PACK = 4
PASS = P * PACK
PASSES = SLOTS // PASS
Q_BLOCKS = QUERIES // P


def tile_attend_silu_gate_kernel(tc, qT, kT, vT, vs, kb, og, offs, out):
    nc = tc.nc
    with ExitStack() as ctx:
        keep = ctx.enter_context(tc.tile_pool(name="keep", bufs=1))
        half = ctx.enter_context(tc.tile_pool(name="half", bufs=2))
        turn_psum = ctx.enter_context(tc.psum_pool(name="turn_psum", bufs=2))
        score_psum = ctx.enter_context(tc.psum_pool(name="score_psum", bufs=4))
        y_psum = ctx.enter_context(tc.psum_pool(name="y_psum", bufs=2))

        offsets = keep.tile([P, SLOTS // 16], U16, name="offsets")
        ident = keep.tile([P, P], F32, name="ident")
        kb_row = keep.tile([P, TOKENS], F32, name="kb_row")
        vs_row = keep.tile([P, TOKENS], F32, name="vs_row")
        k_planes = [keep.tile([P, TOKENS], F32, name="k_plane%d" % j) for j in range(PACK)]
        v_pool = keep.tile([P, TOKENS], F32, name="v_pool")
        q_raw = keep.tile([P, PACK, QUERIES], F32, name="q_raw")
        gate_in = keep.tile([P, Q_BLOCKS, V_FEATURES], F32, name="gate_in")

        k_rows = kT.rearrange("(p j) n -> j p n", j=PACK)

        share = 3 * TOKENS // 4
        for row in (kb_row, vs_row):
            nc.vector.memset(row[:, 0:share], 0.0)
            nc.gpsimd.memset(row[:, share:TOKENS], 0.0)
        make_identity(nc, ident[:])
        nc.scalar.dma_start(gate_in[:], og[0].rearrange("(b p) e -> p b e", p=P))
        nc.sync.dma_start(offsets[:], offs)
        nc.sync.dma_start(k_planes[0][:], k_rows[0])
        nc.sync.dma_start(kb_row[0:1, :], kb[0:1, :])
        nc.sync.dma_start(k_planes[1][:], k_rows[1])
        nc.sync.dma_start(vs_row[0:1, :], vs[0:1, :])
        nc.sync.dma_start(k_planes[2][:], k_rows[2])
        nc.sync.dma_start(q_raw[:], qT[0].rearrange("(p j) q -> p j q", j=PACK))
        nc.sync.dma_start(k_planes[3][:], k_rows[3])
        nc.sync.dma_start(v_pool[:], vT)

        gate = keep.tile([P, Q_BLOCKS, V_FEATURES], F32, name="gate")
        nc.scalar.activation(gate[:], gate_in[:], SIGMOID)
        warm = keep.tile([P, 1], F32, name="warm")
        nc.scalar.activation(warm[:], gate[:, 0, 0:1], SILU)

        k_packed = keep.tile([P, PASSES, PACK, P, PACK], BF16, name="k_packed", align_bytes=64)
        k_codes = keep.tile([P, SLOTS], U32, name="k_codes", align_bytes=64)
        k_scales = keep.tile([P, SLOTS], U8, name="k_scales", align_bytes=64)

        k_picked = keep.tile([P, 2, SLOTS], F32, name="k_picked")

        def gather_keys_plain(j):
            nc.vector.tensor_copy(k_picked[:, j, :], k_planes[j][:].indirect(offsets[:]))

        def interleave_keys(g):
            nc.scalar.copy(
                k_packed[:, g, :, :, 0:2],
                k_picked[:, :, PASS * g : PASS * (g + 1)].rearrange("p j (m t) -> p t m j", t=PACK),
            )

        def gather_keys(j):
            nc.vector.tensor_copy(
                k_packed[:, :, :, :, j].rearrange("p g t m -> p g m t"),
                k_planes[j][:].indirect(offsets[:]),
            )

        def gather_keys_half(j, g):
            nc.vector.tensor_copy(
                k_packed[:, g, :, :, j].rearrange("p t m -> p m t"),
                k_planes[j][:].indirect(offsets[:, 32 * g : 32 * g + 32]),
            )

        def columns(row, name):
            picked = keep.tile([P, SLOTS], F32, name=name + "_picked")
            nc.vector.tensor_copy(picked[:], row[:].indirect(offsets[:]))
            cols = keep.tile([P, PASSES, PACK], F32, name=name + "_cols")
            for g in range(PASSES):
                turned = turn_psum.tile([P, PACK, P], F32, name="turned", tag="turned")
                for t in range(PACK):
                    nc.tensor.transpose(turned[:, t, :], picked[:, PASS * g + t : PASS * (g + 1) : PACK], ident[:])
                nc.scalar.copy(cols[:, g, :], turned[:, :, 0])
            return cols

        gather_keys_plain(0)
        kb_cols = columns(kb_row, "kb")
        gather_keys_plain(1)
        for g in range(PASSES):
            interleave_keys(g)
        vs_cols = columns(vs_row, "vs")
        gather_keys(2)
        q_packed = keep.tile([P, QUERIES, PACK], BF16, name="q_packed", align_bytes=64)
        q_codes = keep.tile([P, QUERIES], U32, name="q_codes", align_bytes=64)
        q_scales = keep.tile([P, QUERIES], U8, name="q_scales", align_bytes=64)
        nc.scalar.copy(q_packed[:], q_raw[:].rearrange("p j q -> p q j"))

        def quantize_keys(g):
            cols = slice(PASS * g, PASS * (g + 1))
            nc.vector.quantize_mx(
                out=k_codes[:, cols].bitcast(FP8X4),
                scales=k_scales[:, cols],
                in_=k_packed[:, g, :, :, :].rearrange("p t m j -> p (t m j)"),
            )

        p_tiles = [half.tile([P, PACK, QUERIES], F32, name="p_tile%d" % g) for g in range(PASSES)]
        v_tiles = [half.tile([P, V_FEATURES, PACK], BF16, name="v_packed%d" % g, align_bytes=64) for g in range(PASSES)]
        w_codes = keep.tile([P, PASSES, QUERIES], U32, name="w_codes", align_bytes=64)
        w_scales = keep.tile([P, PASSES, QUERIES], U8, name="w_scales", align_bytes=64)
        v_codes = keep.tile([P, PASSES, V_FEATURES], U32, name="v_codes", align_bytes=64)
        v_scales = keep.tile([P, PASSES, V_FEATURES], U8, name="v_scales", align_bytes=64)

        def score(g):
            for pair in range(2):
                bank = score_psum.tile([P, 2, QUERIES], F32, name="bank")
                for i in range(2):
                    c0 = PASS * g + P * (2 * pair + i)
                    nc.tensor.matmul_mx(
                        out=bank[:, i, :],
                        lhsT=k_codes[:, c0 : c0 + P].bitcast(FP8X4),
                        lhsT_scale=k_scales[:, c0 : c0 + P],
                        rhs=q_codes[:].bitcast(FP8X4),
                        rhs_scale=q_scales[:],
                        start=True,
                        stop=True,
                    )
                for i in range(2):
                    t = 2 * pair + i
                    nc.scalar.activation(p_tiles[g][:, t, :], bank[:, i, :], SILU, bias=kb_cols[:, g, t : t + 1])

        w_tiles = []

        def weigh(g):
            w_packed = half.tile([P, QUERIES, PACK], BF16, name="w_packed", tag="stage", align_bytes=64)
            w_tiles.append(w_packed)
            nc.vector.tensor_tensor(
                w_packed[:],
                p_tiles[g][:].rearrange("p t q -> p q t"),
                vs_cols[:, g, :].unsqueeze(1).to_broadcast([P, QUERIES, PACK]),
                MULT,
            )

        def quantize_weights(g):
            nc.vector.quantize_mx(
                out=w_codes[:, g, :].bitcast(FP8X4),
                scales=w_scales[:, g, :],
                in_=w_tiles[g][:].rearrange("p q t -> p (q t)"),
            )

        def gather_values(g):
            v_picked = half.tile([P, PASS], F32, name="v_picked", tag="stage", align_bytes=64)
            nc.vector.tensor_copy(v_picked[:], v_pool[:].indirect(offsets[:, 32 * g : 32 * g + 32]))
            turned = turn_psum.tile([P, PACK, P], F32, name="turned_v", tag="turned")
            for t in range(PACK):
                nc.tensor.transpose(turned[:, t, :], v_picked[:, t:PASS:PACK], ident[:])
            nc.scalar.copy(v_tiles[g][:], turned[:].rearrange("p t e -> p e t"))

        def quantize_values(g):
            nc.vector.quantize_mx(
                out=v_codes[:, g, :].bitcast(FP8X4),
                scales=v_scales[:, g, :],
                in_=v_tiles[g][:].rearrange("p e t -> p (e t)"),
            )

        nc.vector.quantize_mx(
            out=q_codes[:].bitcast(FP8X4), scales=q_scales[:], in_=q_packed[:].rearrange("p q j -> p (q j)")
        )
        gather_keys_half(3, 0)
        gather_keys_half(3, 1)
        quantize_keys(0)
        score(0)
        quantize_keys(1)
        score(1)
        gather_values(0)
        gather_values(1)
        weigh(0)
        weigh(1)
        quantize_weights(0)
        quantize_values(0)
        quantize_values(1)
        quantize_weights(1)

        for b in range(Q_BLOCKS):
            q_cols = slice(P * b, P * (b + 1))
            y = y_psum.tile([P, V_FEATURES], F32, name="y")
            for g in range(PASSES):
                nc.tensor.matmul_mx(
                    out=y[:],
                    lhsT=w_codes[:, g, q_cols].bitcast(FP8X4),
                    lhsT_scale=w_scales[:, g, q_cols],
                    rhs=v_codes[:, g, :].bitcast(FP8X4),
                    rhs_scale=v_scales[:, g, :],
                    start=(g == 0),
                    stop=(g == PASSES - 1),
                )
            result = half.tile([P, V_FEATURES], F32, name="result")
            nc.vector.scalar_tensor_tensor(result[:], y[:], 1.0 / 16.0, gate[:, b, :], MULT, MULT)
            queue = nc.sync if b == 0 else nc.scalar
            queue.dma_start(out[0, q_cols, :], result[:])
